import numpy as np
import ml_dtypes


def mxq(x, axis, fmt="e4m3"):
    dtype, down = {"e4m3": (ml_dtypes.float8_e4m3fn, 7), "e5m2": (ml_dtypes.float8_e5m2, 14)}[fmt]
    v = np.moveaxis(np.asarray(x, np.float32).astype(ml_dtypes.bfloat16).astype(np.float64), axis, -1)
    blocks = v.reshape(v.shape[:-1] + (-1, 32))
    amax = np.abs(blocks).max(-1, keepdims=True)
    byte = np.maximum(np.where(amax > 0, np.frexp(amax)[1] - 1 + 127, 0) - down, 1)
    scale = np.exp2(byte - 127.0)
    codes = (blocks / scale).astype(np.float32).astype(dtype).astype(np.float64)
    return np.moveaxis((codes * scale).reshape(v.shape), -1, axis)


WIDE = False


def mx_kscale(k):
    if not WIDE:
        return np.ones(k)
    levels = np.array([10, -10, 5, -5, 0])
    if k % 512:
        return np.exp2(np.random.permutation(np.resize(levels, k // 32))).repeat(32)
    a = np.empty((k // 512, 16))
    for p in range(k // 512):
        a[p, :8] = np.random.permutation(np.resize(levels, 8))
        for g in range(8):
            far = levels[np.abs(levels - a[p, g]) >= 10]
            a[p, g + 8] = far[np.random.randint(len(far))]
    return np.exp2(a.ravel()).repeat(32)


def f64(x):
    return np.asarray(x).astype(np.float64)


def striped8(idx):
    return np.asarray(idx).reshape(8, -1, 16).transpose(0, 2, 1).reshape(128, -1).astype(np.uint16)


def unstriped8(offs):
    return offs.reshape(8, 16, -1).transpose(0, 2, 1).reshape(8, -1).astype(np.int64)


def pick8(x, idx, run):
    r = np.arange(len(x))
    return x[r[:, None], idx[r % (8 * run) // run]]


E2M1 = np.array([0.0, 0.5, 1.0, 1.5, 2.0, 3.0, 4.0, 6.0, -0.0, -0.5, -1.0, -1.5, -2.0, -3.0, -4.0, -6.0])


def pack_weight(w, fmt):
    k, n = w.shape
    w = f64(np.asarray(w, np.float32).astype(ml_dtypes.bfloat16)).reshape(k // 32, 32, n)
    amax = np.abs(w).max(1)
    if fmt == "e4m3":
        byte = np.frexp(amax)[1] - 1 + 127 - 7
    else:
        mant, ex = np.frexp(amax / 6.0)
        byte = np.where(mant > 0.5, ex, ex - 1) + 127
    byte = np.clip(np.where(amax > 0, byte, 1), 1, 254)
    scaled = (w * np.exp2(127.0 - byte)[:, None, :]).reshape(k, n).astype(np.float32)
    by_word = np.ascontiguousarray(scaled.reshape(k // 512, 128, 4, n).transpose(0, 1, 3, 2))
    if fmt == "e4m3":
        words = by_word.astype(ml_dtypes.float8_e4m3fn).view(np.uint8)
    else:
        c = by_word.astype(ml_dtypes.float4_e2m1fn).view(np.uint8) & 0xF
        words = (c[..., 0::2] | (c[..., 1::2] << 4)).reshape(k // 512, 128, 2 * n)
    return np.ascontiguousarray(words), np.ascontiguousarray(byte.astype(np.uint8).reshape(k // 512, 16, n))


def unpack_weight(words, scales, fmt):
    g, _, n = scales.shape
    words = np.ascontiguousarray(words).reshape(g, 128, n, -1)
    if fmt == "e4m3":
        vals = words.view(ml_dtypes.float8_e4m3fn).astype(np.float64)
    else:
        nib = np.empty((g, 128, n, 4), np.uint8)
        nib[..., 0::2] = words & 0xF
        nib[..., 1::2] = words >> 4
        vals = E2M1[nib]
    vals = vals * np.repeat(np.exp2(scales.astype(np.float64) - 127.0), 8, axis=1)[..., None]
    return vals.transpose(0, 1, 3, 2).reshape(g * 512, n)


D, K, T, I, Q = 512, 512, 1024, 512, 128


def setup_inputs():
    n = np.random.standard_normal
    idx = np.stack([np.random.permutation(T)[:I] for _ in range(8)])
    idx2 = np.stack([np.random.permutation(T)[:I] for _ in range(8)])
    idx3 = np.stack([np.random.permutation(T)[:I] for _ in range(8)])
    idx4 = np.stack([np.random.permutation(T)[:I] for _ in range(8)])
    fd = mx_kscale(D)
    fk = mx_kscale(K)
    wqp = pack_weight(n((D, K)) * 1.0 / np.sqrt(D) * fd[:, None] * fk, "e4m3")
    keysp = pack_weight(n((K, T)) * 1.0 / np.sqrt(K) / fk[:, None], "e2m1")
    tagsp = pack_weight(n((D, T)) * 0.5 / np.sqrt(D) * fd[:, None], "e4m3")
    return {
        "states": (n((D, Q)) * 0.95 / fd[:, None]).astype(np.float32),
        "wq_words": wqp[0],
        "wq_scales": wqp[1],
        "keys_words": keysp[0],
        "keys_scales": keysp[1],
        "tags_words": tagsp[0],
        "tags_scales": tagsp[1],
        "offs": striped8(idx),
        "offs2": striped8(idx2),
        "offs3": striped8(idx3),
        "offs4": striped8(idx4),
    }


def reference(states, wq_words, wq_scales, keys_words, keys_scales, tags_words, tags_scales, offs, offs2, offs3, offs4):
    idx = unstriped8(offs)
    idx2 = unstriped8(offs2)
    idx3 = unstriped8(offs3)
    idx4 = unstriped8(offs4)
    wqu = unpack_weight(wq_words, wq_scales, "e4m3")
    keysu = unpack_weight(keys_words, keys_scales, "e2m1")
    tagsu = unpack_weight(tags_words, tags_scales, "e4m3")
    statesq = mxq(f64(states), 0, "e4m3")
    qv = wqu.T @ statesq
    qvq = mxq(qv, 0, "e4m3")
    a = qvq.T @ keysu + statesq.T @ tagsu
    hi1 = np.maximum(pick8(a, idx, 16), pick8(a, idx2, 16))
    lo1 = np.minimum(pick8(a, idx, 16), pick8(a, idx2, 16))
    f1 = np.zeros((Q, T))
    f1[np.arange(Q)[:, None], idx3[np.arange(Q) % 128 // 16]] = hi1
    f2 = np.zeros((Q, T))
    f2[np.arange(Q)[:, None], idx4[np.arange(Q) % 128 // 16]] = lo1
    r = f1 - f2
    cc = a + r
    y = pick8(cc, idx, 16)
    return y

@@ -1,0 +1,162 @@
+from contextlib import ExitStack
+
+import concourse.mybir as mybir
+
+D, K, T, SLOTS, Q = 512, 512, 1024, 512, 128
+FLOPS = 2 * D * K * Q + 2 * K * Q * T + 2 * D * Q * T
+
+F32 = mybir.dt.float32
+BF16 = mybir.dt.bfloat16
+I32 = mybir.dt.int32
+U32 = mybir.dt.uint32
+U16 = mybir.dt.uint16
+U8 = mybir.dt.uint8
+FP8X4 = mybir.dt.float8_e4m3fn_x4
+FP4X4 = mybir.dt.float4_e2m1fn_x4
+ALU = mybir.AluOpType
+COPY = mybir.ActivationFunctionType.Copy
+
+P = 128
+PACK = 4
+LIST_COLS = SLOTS // 16
+HALF = SLOTS // 2
+BANK_T = 256
+
+
+def load_scale_rows(queue, plane, rows):
+    for quadrant in range(4):
+        queue.dma_start(
+            out=plane[:].bitcast(I32)[32 * quadrant : 32 * quadrant + 4, :],
+            in_=rows[0].bitcast(I32)[4 * quadrant : 4 * quadrant + 4, :],
+        )
+
+
+def tile_attend_highlow_madeparts_kernel(
+    tc, states, wq_words, wq_scales, keys_words, keys_scales, tags_words, tags_scales, offs, offs2, offs3, offs4, out
+):
+    nc = tc.nc
+    with ExitStack() as ctx:
+        sb = ctx.enter_context(tc.tile_pool(name="sb", bufs=1))
+        psum = ctx.enter_context(tc.psum_pool(name="psum", bufs=1))
+
+        wq_sc_raw = sb.tile([P, K], U8, align_bytes=64)
+        keys_sc = sb.tile([P, T], U8, align_bytes=64)
+        tags_sc = sb.tile([P, T], U8, align_bytes=64)
+        nc.vector.memset(wq_sc_raw[:].bitcast(I32), 0)
+        nc.gpsimd.memset(tags_sc[:].bitcast(I32), 0)
+        nc.gpsimd.memset(keys_sc[:].bitcast(I32), 0)
+
+        states_raw = sb.tile([P, PACK, Q], F32, align_bytes=64)
+        wq_raw = sb.tile([P, K], U32, align_bytes=64)
+        tags_w = sb.tile([P, T], U32, align_bytes=64)
+        keys_w = sb.tile([P, 2 * T], U8, align_bytes=64)
+        load_scale_rows(nc.scalar, wq_sc_raw, wq_scales)
+        nc.sync.dma_start(out=states_raw[:], in_=states.rearrange("(p j) q -> p j q", j=PACK))
+        nc.sync.dma_start(out=wq_raw[:].bitcast(I32), in_=wq_words[0].rearrange("p n t -> p (n t)").bitcast(I32))
+        nc.sync.dma_start(out=keys_w[:].bitcast(I32), in_=keys_words[0].bitcast(I32))
+        nc.sync.dma_start(out=tags_w[:].bitcast(I32), in_=tags_words[0].rearrange("p n t -> p (n t)").bitcast(I32))
+        load_scale_rows(nc.sync, tags_sc, tags_scales)
+        load_scale_rows(nc.sync, keys_sc, keys_scales)
+        lists = []
+        for name, src in (("idx", offs), ("idx2", offs2), ("idx3", offs3), ("idx4", offs4)):
+            tile = sb.tile([P, LIST_COLS], U16, name=name)
+            nc.sync.dma_start(tile[:], src)
+            lists.append(tile)
+        idx, idx2, idx3, idx4 = lists
+
+        f1 = sb.tile([P, T], F32, align_bytes=64)
+        f2 = sb.tile([P, T], F32, align_bytes=64)
+        nc.vector.memset(f1[:], 0.0)
+        nc.vector.memset(f2[:], 0.0)
+
+        wq_sc = sb.tile([P, K], U8, align_bytes=64)
+        nc.vector.tensor_copy(
+            out=wq_sc[:].rearrange("p (t m) -> p m t", t=PACK), in_=wq_sc_raw[:].rearrange("p (m t) -> p m t", t=PACK)
+        )
+        wq_w = sb.tile([P, K], U32, align_bytes=64)
+        nc.scalar.copy(
+            out=wq_w[:].rearrange("p (t m) -> p m t", t=PACK), in_=wq_raw[:].rearrange("p (m t) -> p m t", t=PACK)
+        )
+
+        states_bf = sb.tile([P, Q * PACK], BF16, align_bytes=64)
+        nc.vector.tensor_copy(
+            out=states_bf[:].rearrange("p (c i j) -> p c j i", i=4, j=PACK),
+            in_=states_raw[:].rearrange("p j (c i) -> p c j i", i=4),
+        )
+        states_w = sb.tile([P, Q], U32, align_bytes=64)
+        states_sc = sb.tile([P, Q], U8, align_bytes=64)
+        nc.vector.quantize_mx(out=states_w[:].bitcast(FP8X4), scales=states_sc[:], in_=states_bf[:])
+
+        qv_ps = psum.tile([P, PACK, Q], F32)
+        for t in range(PACK):
+            cols = slice(t * P, (t + 1) * P)
+            nc.tensor.matmul_mx(
+                out=qv_ps[:, t, :],
+                lhsT=wq_w[:, cols].bitcast(FP8X4),
+                lhsT_scale=wq_sc[:, cols],
+                rhs=states_w[:].bitcast(FP8X4),
+                rhs_scale=states_sc[:],
+                start=True,
+                stop=True,
+            )
+        qv_bf = sb.tile([P, Q * PACK], BF16, align_bytes=64)
+        nc.scalar.copy(out=qv_bf[:].rearrange("p (q t) -> p q t", t=PACK), in_=qv_ps[:].rearrange("p t q -> p q t"))
+        qv_w = sb.tile([P, Q], U32, align_bytes=64)
+        qv_sc = sb.tile([P, Q], U8, align_bytes=64)
+        nc.vector.quantize_mx(out=qv_w[:].bitcast(FP8X4), scales=qv_sc[:], in_=qv_bf[:])
+
+        banks = [psum.tile([P, BANK_T], F32, name=f"scores{b}") for b in range(T // BANK_T)]
+        for b, bank in enumerate(banks):
+            cols = slice(b * BANK_T, (b + 1) * BANK_T)
+            nc.tensor.matmul_mx(
+                out=bank[:],
+                lhsT=states_w[:].bitcast(FP8X4),
+                lhsT_scale=states_sc[:],
+                rhs=tags_w[:, cols].bitcast(FP8X4),
+                rhs_scale=tags_sc[:, cols],
+                start=True,
+                stop=False,
+            )
+        a = sb.tile([P, T], F32, align_bytes=64)
+        for b, bank in enumerate(banks):
+            cols = slice(b * BANK_T, (b + 1) * BANK_T)
+            nc.tensor.matmul_mx(
+                out=bank[:],
+                lhsT=qv_w[:].bitcast(FP8X4),
+                lhsT_scale=qv_sc[:],
+                rhs=keys_w[:, 2 * cols.start : 2 * cols.stop].bitcast(FP4X4),
+                rhs_scale=keys_sc[:, cols],
+                start=False,
+                stop=True,
+            )
+            if b % 2 == 0:
+                nc.scalar.copy(out=a[:, cols], in_=bank[:])
+            else:
+                nc.vector.tensor_copy(out=a[:, cols], in_=bank[:])
+
+        halves = [slice(h * LIST_COLS // 2, (h + 1) * LIST_COLS // 2) for h in range(2)]
+        x = [sb.tile([P, HALF], F32, name=f"x{h}") for h in range(2)]
+        y = [sb.tile([P, HALF], F32, name=f"y{h}") for h in range(2)]
+        hi = [sb.tile([P, HALF], F32, name=f"hi{h}") for h in range(2)]
+        lo = [sb.tile([P, HALF], F32, name=f"lo{h}") for h in range(2)]
+        nc.vector.tensor_copy(x[0][:], a[:].indirect(idx[:, halves[0]]))
+        nc.scalar.activation(y[0][:], a[:].indirect(idx2[:, halves[0]]), COPY)
+        nc.scalar.activation(x[1][:], a[:].indirect(idx[:, halves[1]]), COPY)
+        nc.scalar.activation(y[1][:], a[:].indirect(idx2[:, halves[1]]), COPY)
+        for h in range(2):
+            nc.vector.tensor_tensor(hi[h][:], x[h][:], y[h][:], ALU.max)
+            nc.vector.tensor_tensor(lo[h][:], x[h][:], y[h][:], ALU.min)
+            nc.vector.tensor_copy(f1[:].indirect(idx3[:, halves[h]]), hi[h][:])
+        for h in range(2):
+            nc.vector.tensor_copy(f2[:].indirect(idx4[:, halves[h]]), lo[h][:])
+
+        a_f1 = sb.tile([P, T], F32, align_bytes=64)
+        nc.gpsimd.tensor_tensor(a_f1[:], a[:], f1[:], ALU.add)
+        cc = sb.tile([P, T], F32, align_bytes=64)
+        nc.vector.tensor_tensor(cc[:], a_f1[:], f2[:], ALU.subtract)
+
+        res = [sb.tile([P, HALF], F32, name=f"res{h}") for h in range(2)]
+        nc.vector.tensor_copy(res[0][:], cc[:].indirect(idx[:, halves[0]]))
+        nc.scalar.activation(res[1][:], cc[:].indirect(idx[:, halves[1]]), COPY)
+        nc.sync.dma_start(out=out[:, 0:HALF], in_=res[0][:])
+        nc.scalar.dma_start(out=out[:, HALF:SLOTS], in_=res[1][:])

@@ -20,11 +20,11 @@ P = 128
 PACK = 4
 LIST_COLS = SLOTS // 16
 HALF = SLOTS // 2
-BANK_T = 256
+BANK_WIDTHS = (256, 256, 256, 128, 128)
 
 
-def load_scale_rows(queue, plane, rows):
-    for quadrant in range(4):
+def load_scale_rows(queue, plane, rows, quadrants):
+    for quadrant in quadrants:
         queue.dma_start(
             out=plane[:].bitcast(I32)[32 * quadrant : 32 * quadrant + 4, :],
             in_=rows[0].bitcast(I32)[4 * quadrant : 4 * quadrant + 4, :],
@@ -42,7 +42,7 @@ def tile_attend_highlow_madeparts_kernel(
         wq_sc_raw = sb.tile([P, K], U8, align_bytes=64)
         keys_sc = sb.tile([P, T], U8, align_bytes=64)
         tags_sc = sb.tile([P, T], U8, align_bytes=64)
-        nc.vector.memset(wq_sc_raw[:].bitcast(I32), 0)
+        nc.gpsimd.memset(wq_sc_raw[:].bitcast(I32), 0)
         nc.gpsimd.memset(tags_sc[:].bitcast(I32), 0)
         nc.gpsimd.memset(keys_sc[:].bitcast(I32), 0)
 
@@ -50,13 +50,15 @@ def tile_attend_highlow_madeparts_kernel(
         wq_raw = sb.tile([P, K], U32, align_bytes=64)
         tags_w = sb.tile([P, T], U32, align_bytes=64)
         keys_w = sb.tile([P, 2 * T], U8, align_bytes=64)
-        load_scale_rows(nc.scalar, wq_sc_raw, wq_scales)
         nc.sync.dma_start(out=states_raw[:], in_=states.rearrange("(p j) q -> p j q", j=PACK))
         nc.sync.dma_start(out=wq_raw[:].bitcast(I32), in_=wq_words[0].rearrange("p n t -> p (n t)").bitcast(I32))
-        nc.sync.dma_start(out=keys_w[:].bitcast(I32), in_=keys_words[0].bitcast(I32))
+        load_scale_rows(nc.sync, wq_sc_raw, wq_scales, range(4))
+        load_scale_rows(nc.sync, tags_sc, tags_scales, range(1))
         nc.sync.dma_start(out=tags_w[:].bitcast(I32), in_=tags_words[0].rearrange("p n t -> p (n t)").bitcast(I32))
-        load_scale_rows(nc.sync, tags_sc, tags_scales)
-        load_scale_rows(nc.sync, keys_sc, keys_scales)
+        load_scale_rows(nc.sync, tags_sc, tags_scales, range(1, 4))
+        load_scale_rows(nc.sync, keys_sc, keys_scales, range(1))
+        nc.sync.dma_start(out=keys_w[:].bitcast(I32), in_=keys_words[0].bitcast(I32))
+        load_scale_rows(nc.sync, keys_sc, keys_scales, range(1, 4))
         lists = []
         for name, src in (("idx", offs), ("idx2", offs2), ("idx3", offs3), ("idx4", offs4)):
             tile = sb.tile([P, LIST_COLS], U16, name=name)
@@ -105,9 +107,10 @@ def tile_attend_highlow_madeparts_kernel(
         qv_sc = sb.tile([P, Q], U8, align_bytes=64)
         nc.vector.quantize_mx(out=qv_w[:].bitcast(FP8X4), scales=qv_sc[:], in_=qv_bf[:])
 
-        banks = [psum.tile([P, BANK_T], F32, name=f"scores{b}") for b in range(T // BANK_T)]
+        banks = [psum.tile([P, w], F32, name=f"scores{b}") for b, w in enumerate(BANK_WIDTHS)]
+        bank_cols = [slice(sum(BANK_WIDTHS[:b]), sum(BANK_WIDTHS[: b + 1])) for b in range(len(BANK_WIDTHS))]
         for b, bank in enumerate(banks):
-            cols = slice(b * BANK_T, (b + 1) * BANK_T)
+            cols = bank_cols[b]
             nc.tensor.matmul_mx(
                 out=bank[:],
                 lhsT=states_w[:].bitcast(FP8X4),
@@ -119,7 +122,7 @@ def tile_attend_highlow_madeparts_kernel(
             )
         a = sb.tile([P, T], F32, align_bytes=64)
         for b, bank in enumerate(banks):
-            cols = slice(b * BANK_T, (b + 1) * BANK_T)
+            cols = bank_cols[b]
             nc.tensor.matmul_mx(
                 out=bank[:],
                 lhsT=qv_w[:].bitcast(FP8X4),
@@ -136,19 +139,21 @@ def tile_attend_highlow_madeparts_kernel(
 
         halves = [slice(h * LIST_COLS // 2, (h + 1) * LIST_COLS // 2) for h in range(2)]
         x = [sb.tile([P, HALF], F32, name=f"x{h}") for h in range(2)]
-        y = [sb.tile([P, HALF], F32, name=f"y{h}") for h in range(2)]
+        y = [sb.tile([P, HALF], F32, name="y")]
         hi = [sb.tile([P, HALF], F32, name=f"hi{h}") for h in range(2)]
-        lo = [sb.tile([P, HALF], F32, name=f"lo{h}") for h in range(2)]
+        lo_all = sb.tile([P, SLOTS], F32)
+        lo = [lo_all[:, h * HALF : (h + 1) * HALF] for h in range(2)]
         nc.vector.tensor_copy(x[0][:], a[:].indirect(idx[:, halves[0]]))
         nc.scalar.activation(y[0][:], a[:].indirect(idx2[:, halves[0]]), COPY)
         nc.scalar.activation(x[1][:], a[:].indirect(idx[:, halves[1]]), COPY)
-        nc.scalar.activation(y[1][:], a[:].indirect(idx2[:, halves[1]]), COPY)
         for h in range(2):
+            if h == 1:
+                y.append(sb.tile([P, HALF], F32, name="y"))
+                nc.scalar.activation(y[1][:], a[:].indirect(idx2[:, halves[1]]), COPY)
             nc.vector.tensor_tensor(hi[h][:], x[h][:], y[h][:], ALU.max)
-            nc.vector.tensor_tensor(lo[h][:], x[h][:], y[h][:], ALU.min)
+            nc.vector.tensor_tensor(lo[h], x[h][:], y[h][:], ALU.min)
             nc.vector.tensor_copy(f1[:].indirect(idx3[:, halves[h]]), hi[h][:])
-        for h in range(2):
-            nc.vector.tensor_copy(f2[:].indirect(idx4[:, halves[h]]), lo[h][:])
+        nc.vector.tensor_copy(f2[:].indirect(idx4[:]), lo_all[:])
 
         a_f1 = sb.tile([P, T], F32, align_bytes=64)
         nc.gpsimd.tensor_tensor(a_f1[:], a[:], f1[:], ALU.add)

@@ -1,6 +1,7 @@
 from contextlib import ExitStack
 
 import concourse.mybir as mybir
+from concourse.masks import make_identity
 
 D, K, T, SLOTS, Q = 512, 512, 1024, 512, 128
 FLOPS = 2 * D * K * Q + 2 * K * Q * T + 2 * D * Q * T
@@ -71,6 +72,9 @@ def tile_attend_highlow_madeparts_kernel(
         nc.vector.memset(f1[:], 0.0)
         nc.vector.memset(f2[:], 0.0)
 
+        ident = sb.tile([P, P], F32, align_bytes=64)
+        make_identity(nc, ident[:])
+
         wq_sc = sb.tile([P, K], U8, align_bytes=64)
         nc.vector.tensor_copy(
             out=wq_sc[:].rearrange("p (t m) -> p m t", t=PACK), in_=wq_sc_raw[:].rearrange("p (m t) -> p m t", t=PACK)
@@ -107,7 +111,7 @@ def tile_attend_highlow_madeparts_kernel(
         qv_sc = sb.tile([P, Q], U8, align_bytes=64)
         nc.vector.quantize_mx(out=qv_w[:].bitcast(FP8X4), scales=qv_sc[:], in_=qv_bf[:])
 
-        banks = [psum.tile([P, w], F32, name=f"scores{b}") for b, w in enumerate(BANK_WIDTHS)]
+        banks = [psum.tile([P, w], F32, name=f"scores{b}", tag=f"scores{b}") for b, w in enumerate(BANK_WIDTHS)]
         bank_cols = [slice(sum(BANK_WIDTHS[:b]), sum(BANK_WIDTHS[: b + 1])) for b in range(len(BANK_WIDTHS))]
         for b, bank in enumerate(banks):
             cols = bank_cols[b]
@@ -155,10 +159,24 @@ def tile_attend_highlow_madeparts_kernel(
             nc.vector.tensor_copy(f1[:].indirect(idx3[:, halves[h]]), hi[h][:])
         nc.vector.tensor_copy(f2[:].indirect(idx4[:]), lo_all[:])
 
-        a_f1 = sb.tile([P, T], F32, align_bytes=64)
-        nc.gpsimd.tensor_tensor(a_f1[:], a[:], f1[:], ALU.add)
+        turned = sb.tile([P, T], F32, align_bytes=64)
+        a_f1 = [psum.tile([P, 512], F32, name=f"back{b}") for b in range(2)]
+        fwd = [psum.tile([P, 256], F32, name=f"fwd{b}", tag=f"scores{b}") for b in range(4)]
+        for b in range(4):
+            for j in range(2):
+                cols = slice(256 * b + P * j, 256 * b + P * (j + 1))
+                nc.tensor.matmul(fwd[b][:, P * j : P * (j + 1)], a[:, cols], ident[:], start=(j == 0), stop=False, is_transpose=True)
+        for b in range(4):
+            for j in range(2):
+                cols = slice(256 * b + P * j, 256 * b + P * (j + 1))
+                nc.tensor.matmul(fwd[b][:, P * j : P * (j + 1)], f1[:, cols], ident[:], start=False, stop=(j == 1), is_transpose=True)
+            nc.scalar.copy(out=turned[:, 256 * b : 256 * (b + 1)], in_=fwd[b][:])
+        for c in range(8):
+            nc.tensor.transpose(a_f1[c // 4][:, P * (c % 4) : P * (c % 4 + 1)], turned[:, P * c : P * (c + 1)], ident[:])
         cc = sb.tile([P, T], F32, align_bytes=64)
-        nc.vector.tensor_tensor(cc[:], a_f1[:], f2[:], ALU.subtract)
+        for b in range(2):
+            cols = slice(512 * b, 512 * (b + 1))
+            nc.vector.tensor_tensor(cc[:, cols], a_f1[b][:], f2[:, cols], ALU.subtract)
 
         res = [sb.tile([P, HALF], F32, name=f"res{h}") for h in range(2)]
         nc.vector.tensor_copy(res[0][:], cc[:].indirect(idx[:, halves[0]]))

@@ -24,10 +24,10 @@ HALF = SLOTS // 2
 BANK_WIDTHS = (256, 256, 256, 128, 128)
 
 
-def load_scale_rows(queue, plane, rows, quadrants):
+def load_scale_rows(queue, plane, rows, quadrants, first=0):
     for quadrant in quadrants:
         queue.dma_start(
-            out=plane[:].bitcast(I32)[32 * quadrant : 32 * quadrant + 4, :],
+            out=plane[:].bitcast(I32)[32 * quadrant + first : 32 * quadrant + first + 4, :],
             in_=rows[0].bitcast(I32)[4 * quadrant : 4 * quadrant + 4, :],
         )
 
@@ -40,12 +40,12 @@ def tile_attend_highlow_madeparts_kernel(
         sb = ctx.enter_context(tc.tile_pool(name="sb", bufs=1))
         psum = ctx.enter_context(tc.psum_pool(name="psum", bufs=1))
 
-        wq_sc_raw = sb.tile([P, K], U8, align_bytes=64)
+        wq_sc_raw = sb.tile([P, K], U8, align_bytes=64, tag="wq_sc_raw_then_f1")
         keys_sc = sb.tile([P, T], U8, align_bytes=64)
         tags_sc = sb.tile([P, T], U8, align_bytes=64)
         nc.gpsimd.memset(wq_sc_raw[:].bitcast(I32), 0)
         nc.gpsimd.memset(tags_sc[:].bitcast(I32), 0)
-        nc.gpsimd.memset(keys_sc[:].bitcast(I32), 0)
+        nc.vector.memset(keys_sc[:].bitcast(I32), 0)
 
         states_raw = sb.tile([P, PACK, Q], F32, align_bytes=64)
         wq_raw = sb.tile([P, K], U32, align_bytes=64)
@@ -53,10 +53,11 @@ def tile_attend_highlow_madeparts_kernel(
         keys_w = sb.tile([P, 2 * T], U8, align_bytes=64)
         nc.sync.dma_start(out=states_raw[:], in_=states.rearrange("(p j) q -> p j q", j=PACK))
         nc.sync.dma_start(out=wq_raw[:].bitcast(I32), in_=wq_words[0].rearrange("p n t -> p (n t)").bitcast(I32))
-        load_scale_rows(nc.sync, wq_sc_raw, wq_scales, range(4))
-        load_scale_rows(nc.sync, tags_sc, tags_scales, range(1))
+        load_scale_rows(nc.sync, wq_sc_raw, wq_scales, range(4), 4)
+        load_scale_rows(nc.gpsimd, tags_sc, tags_scales, range(3, 4), 8)
+        load_scale_rows(nc.sync, tags_sc, tags_scales, range(1), 8)
         nc.sync.dma_start(out=tags_w[:].bitcast(I32), in_=tags_words[0].rearrange("p n t -> p (n t)").bitcast(I32))
-        load_scale_rows(nc.sync, tags_sc, tags_scales, range(1, 4))
+        load_scale_rows(nc.sync, tags_sc, tags_scales, range(1, 3), 8)
         load_scale_rows(nc.sync, keys_sc, keys_scales, range(1))
         nc.sync.dma_start(out=keys_w[:].bitcast(I32), in_=keys_words[0].bitcast(I32))
         load_scale_rows(nc.sync, keys_sc, keys_scales, range(1, 4))
@@ -67,17 +68,17 @@ def tile_attend_highlow_madeparts_kernel(
             lists.append(tile)
         idx, idx2, idx3, idx4 = lists
 
-        f1 = sb.tile([P, T], F32, align_bytes=64)
-        f2 = sb.tile([P, T], F32, align_bytes=64)
-        nc.vector.memset(f1[:], 0.0)
-        nc.vector.memset(f2[:], 0.0)
 
         ident = sb.tile([P, P], F32, align_bytes=64)
-        make_identity(nc, ident[:])
+        nc.vector.memset(ident[:], 0.0)
+        make_identity(nc, ident[:], nomemset=True)
+        f2 = sb.tile([P, T], F32, align_bytes=64)
+        nc.vector.memset(f2[:, 0 : T - 1], 0.0)
+        nc.vector.memset(f2[:, T - 1 : T], 0.0)
 
         wq_sc = sb.tile([P, K], U8, align_bytes=64)
         nc.vector.tensor_copy(
-            out=wq_sc[:].rearrange("p (t m) -> p m t", t=PACK), in_=wq_sc_raw[:].rearrange("p (m t) -> p m t", t=PACK)
+            out=wq_sc[:].rearrange("p (t m) -> p t m", t=PACK), in_=wq_sc_raw[:].rearrange("p (m t) -> p t m", t=PACK)
         )
         wq_w = sb.tile([P, K], U32, align_bytes=64)
         nc.scalar.copy(
@@ -93,13 +94,16 @@ def tile_attend_highlow_madeparts_kernel(
         states_sc = sb.tile([P, Q], U8, align_bytes=64)
         nc.vector.quantize_mx(out=states_w[:].bitcast(FP8X4), scales=states_sc[:], in_=states_bf[:])
 
+        f1 = sb.tile([P, T], F32, align_bytes=64, tag="wq_sc_raw_then_f1")
+        nc.vector.memset(f1[:], 0.0)
+
         qv_ps = psum.tile([P, PACK, Q], F32)
         for t in range(PACK):
             cols = slice(t * P, (t + 1) * P)
             nc.tensor.matmul_mx(
                 out=qv_ps[:, t, :],
                 lhsT=wq_w[:, cols].bitcast(FP8X4),
-                lhsT_scale=wq_sc[:, cols],
+                lhsT_scale=wq_sc[4:P, cols],
                 rhs=states_w[:].bitcast(FP8X4),
                 rhs_scale=states_sc[:],
                 start=True,
@@ -120,7 +124,7 @@ def tile_attend_highlow_madeparts_kernel(
                 lhsT=states_w[:].bitcast(FP8X4),
                 lhsT_scale=states_sc[:],
                 rhs=tags_w[:, cols].bitcast(FP8X4),
-                rhs_scale=tags_sc[:, cols],
+                rhs_scale=tags_sc[8:P, cols],
                 start=True,
                 stop=False,
             )
@@ -159,24 +163,26 @@ def tile_attend_highlow_madeparts_kernel(
             nc.vector.tensor_copy(f1[:].indirect(idx3[:, halves[h]]), hi[h][:])
         nc.vector.tensor_copy(f2[:].indirect(idx4[:]), lo_all[:])
 
-        turned = sb.tile([P, T], F32, align_bytes=64)
+        turned = sb.tile([P, 768], F32, align_bytes=64)
         a_f1 = [psum.tile([P, 512], F32, name=f"back{b}") for b in range(2)]
-        fwd = [psum.tile([P, 256], F32, name=f"fwd{b}", tag=f"scores{b}") for b in range(4)]
-        for b in range(4):
+        fwd = [psum.tile([P, 256], F32, name=f"fwd{b}", tag=f"scores{b}") for b in range(3)]
+        for b in range(3):
             for j in range(2):
                 cols = slice(256 * b + P * j, 256 * b + P * (j + 1))
                 nc.tensor.matmul(fwd[b][:, P * j : P * (j + 1)], a[:, cols], ident[:], start=(j == 0), stop=False, is_transpose=True)
-        for b in range(4):
+        for b in range(3):
             for j in range(2):
                 cols = slice(256 * b + P * j, 256 * b + P * (j + 1))
                 nc.tensor.matmul(fwd[b][:, P * j : P * (j + 1)], f1[:, cols], ident[:], start=False, stop=(j == 1), is_transpose=True)
             nc.scalar.copy(out=turned[:, 256 * b : 256 * (b + 1)], in_=fwd[b][:])
-        for c in range(8):
+        for c in range(6):
             nc.tensor.transpose(a_f1[c // 4][:, P * (c % 4) : P * (c % 4 + 1)], turned[:, P * c : P * (c + 1)], ident[:])
         cc = sb.tile([P, T], F32, align_bytes=64)
-        for b in range(2):
-            cols = slice(512 * b, 512 * (b + 1))
-            nc.vector.tensor_tensor(cc[:, cols], a_f1[b][:], f2[:, cols], ALU.subtract)
+        a_f1_rest = sb.tile([P, 256], F32, align_bytes=64)
+        nc.gpsimd.tensor_tensor(a_f1_rest[:], a[:, 768:T], f1[:, 768:T], ALU.add)
+        nc.gpsimd.tensor_tensor(cc[:, 768:T], a_f1_rest[:], f2[:, 768:T], ALU.subtract)
+        nc.vector.tensor_tensor(cc[:, 0:512], a_f1[0][:], f2[:, 0:512], ALU.subtract)
+        nc.vector.tensor_tensor(cc[:, 512:768], a_f1[1][:, 0:256], f2[:, 512:768], ALU.subtract)
 
         res = [sb.tile([P, HALF], F32, name=f"res{h}") for h in range(2)]
         nc.vector.tensor_copy(res[0][:], cc[:].indirect(idx[:, halves[0]]))

@@ -19,17 +19,30 @@ COPY = mybir.ActivationFunctionType.Copy
 
 P = 128
 PACK = 4
+QUADRANT = 32
+QUADRANT_ROWS = 4
+PSUM_BANK = 512
 LIST_COLS = SLOTS // 16
 HALF = SLOTS // 2
-BANK_WIDTHS = (256, 256, 256, 128, 128)
+
+WQ_FIRST, TAGS_FIRST, KEYS_FIRST = 4, 8, 0
+
+SCALAR_DEAL = 48
+SCORE_WIDTHS = (256, 256, 256, 128, 128)
+VECTOR_COLS = 768
+TURN_COLS = 256
 
 
-def load_scale_rows(queue, plane, rows, quadrants, first=0):
-    for quadrant in quadrants:
+def load_scale_rows(queue, plane, scales, quadrants, first):
+    for g in quadrants:
         queue.dma_start(
-            out=plane[:].bitcast(I32)[32 * quadrant + first : 32 * quadrant + first + 4, :],
-            in_=rows[0].bitcast(I32)[4 * quadrant : 4 * quadrant + 4, :],
+            out=plane[:].bitcast(I32)[QUADRANT * g + first : QUADRANT * g + first + QUADRANT_ROWS, :],
+            in_=scales[0].bitcast(I32)[QUADRANT_ROWS * g : QUADRANT_ROWS * (g + 1), :],
         )
+
+
+def fp8_words(words):
+    return words[0].rearrange("p n t -> p (n t)").bitcast(I32)
 
 
 def tile_attend_highlow_madeparts_kernel(
@@ -40,7 +53,7 @@ def tile_attend_highlow_madeparts_kernel(
         sb = ctx.enter_context(tc.tile_pool(name="sb", bufs=1))
         psum = ctx.enter_context(tc.psum_pool(name="psum", bufs=1))
 
-        wq_sc_raw = sb.tile([P, K], U8, align_bytes=64, tag="wq_sc_raw_then_f1")
+        wq_sc_raw = sb.tile([P, K], U8, align_bytes=64)
         keys_sc = sb.tile([P, T], U8, align_bytes=64)
         tags_sc = sb.tile([P, T], U8, align_bytes=64)
         nc.gpsimd.memset(wq_sc_raw[:].bitcast(I32), 0)
@@ -48,26 +61,25 @@ def tile_attend_highlow_madeparts_kernel(
         nc.vector.memset(keys_sc[:].bitcast(I32), 0)
 
         states_raw = sb.tile([P, PACK, Q], F32, align_bytes=64)
-        wq_raw = sb.tile([P, K], U32, align_bytes=64)
+        wq_raw = sb.tile([P, K], U32, align_bytes=64, tag="wq_raw_then_f1")
         tags_w = sb.tile([P, T], U32, align_bytes=64)
         keys_w = sb.tile([P, 2 * T], U8, align_bytes=64)
         nc.sync.dma_start(out=states_raw[:], in_=states.rearrange("(p j) q -> p j q", j=PACK))
-        nc.sync.dma_start(out=wq_raw[:].bitcast(I32), in_=wq_words[0].rearrange("p n t -> p (n t)").bitcast(I32))
-        load_scale_rows(nc.sync, wq_sc_raw, wq_scales, range(4), 4)
-        load_scale_rows(nc.gpsimd, tags_sc, tags_scales, range(3, 4), 8)
-        load_scale_rows(nc.sync, tags_sc, tags_scales, range(1), 8)
-        nc.sync.dma_start(out=tags_w[:].bitcast(I32), in_=tags_words[0].rearrange("p n t -> p (n t)").bitcast(I32))
-        load_scale_rows(nc.sync, tags_sc, tags_scales, range(1, 3), 8)
-        load_scale_rows(nc.sync, keys_sc, keys_scales, range(1))
+        load_scale_rows(nc.sync, wq_sc_raw, wq_scales, (0, 1, 2, 3), WQ_FIRST)
+        nc.sync.dma_start(out=wq_raw[:].bitcast(I32), in_=fp8_words(wq_words))
+        load_scale_rows(nc.gpsimd, tags_sc, tags_scales, (3,), TAGS_FIRST)
+        load_scale_rows(nc.sync, tags_sc, tags_scales, (0,), TAGS_FIRST)
+        nc.sync.dma_start(out=tags_w[:].bitcast(I32), in_=fp8_words(tags_words))
+        load_scale_rows(nc.sync, tags_sc, tags_scales, (1, 2), TAGS_FIRST)
+        load_scale_rows(nc.sync, keys_sc, keys_scales, (0,), KEYS_FIRST)
         nc.sync.dma_start(out=keys_w[:].bitcast(I32), in_=keys_words[0].bitcast(I32))
-        load_scale_rows(nc.sync, keys_sc, keys_scales, range(1, 4))
+        load_scale_rows(nc.sync, keys_sc, keys_scales, (1, 2, 3), KEYS_FIRST)
         lists = []
         for name, src in (("idx", offs), ("idx2", offs2), ("idx3", offs3), ("idx4", offs4)):
-            tile = sb.tile([P, LIST_COLS], U16, name=name)
-            nc.sync.dma_start(tile[:], src)
-            lists.append(tile)
+            list_tile = sb.tile([P, LIST_COLS], U16, name=name)
+            nc.sync.dma_start(list_tile[:], src)
+            lists.append(list_tile)
         idx, idx2, idx3, idx4 = lists
-
 
         ident = sb.tile([P, P], F32, align_bytes=64)
         nc.vector.memset(ident[:], 0.0)
@@ -81,9 +93,9 @@ def tile_attend_highlow_madeparts_kernel(
             out=wq_sc[:].rearrange("p (t m) -> p t m", t=PACK), in_=wq_sc_raw[:].rearrange("p (m t) -> p t m", t=PACK)
         )
         wq_w = sb.tile([P, K], U32, align_bytes=64)
-        nc.scalar.copy(
-            out=wq_w[:].rearrange("p (t m) -> p m t", t=PACK), in_=wq_raw[:].rearrange("p (m t) -> p m t", t=PACK)
-        )
+        dealt = wq_w[:].rearrange("p (t m) -> p m t", t=PACK)
+        undealt = wq_raw[:].rearrange("p (m t) -> p m t", t=PACK)
+        nc.scalar.copy(out=dealt[:, 0:SCALAR_DEAL, :], in_=undealt[:, 0:SCALAR_DEAL, :])
 
         states_bf = sb.tile([P, Q * PACK], BF16, align_bytes=64)
         nc.vector.tensor_copy(
@@ -94,16 +106,20 @@ def tile_attend_highlow_madeparts_kernel(
         states_sc = sb.tile([P, Q], U8, align_bytes=64)
         nc.vector.quantize_mx(out=states_w[:].bitcast(FP8X4), scales=states_sc[:], in_=states_bf[:])
 
-        f1 = sb.tile([P, T], F32, align_bytes=64, tag="wq_sc_raw_then_f1")
+        nc.vector.tensor_copy(
+            out=dealt[:, SCALAR_DEAL:P, :].bitcast(I32), in_=undealt[:, SCALAR_DEAL:P, :].bitcast(I32)
+        )
+
+        f1 = sb.tile([P, T], F32, align_bytes=64, tag="wq_raw_then_f1")
         nc.vector.memset(f1[:], 0.0)
 
         qv_ps = psum.tile([P, PACK, Q], F32)
         for t in range(PACK):
-            cols = slice(t * P, (t + 1) * P)
+            places = slice(t * P, (t + 1) * P)
             nc.tensor.matmul_mx(
                 out=qv_ps[:, t, :],
-                lhsT=wq_w[:, cols].bitcast(FP8X4),
-                lhsT_scale=wq_sc[4:P, cols],
+                lhsT=wq_w[:, places].bitcast(FP8X4),
+                lhsT_scale=wq_sc[WQ_FIRST:P, places],
                 rhs=states_w[:].bitcast(FP8X4),
                 rhs_scale=states_sc[:],
                 start=True,
@@ -115,28 +131,26 @@ def tile_attend_highlow_madeparts_kernel(
         qv_sc = sb.tile([P, Q], U8, align_bytes=64)
         nc.vector.quantize_mx(out=qv_w[:].bitcast(FP8X4), scales=qv_sc[:], in_=qv_bf[:])
 
-        banks = [psum.tile([P, w], F32, name=f"scores{b}", tag=f"scores{b}") for b, w in enumerate(BANK_WIDTHS)]
-        bank_cols = [slice(sum(BANK_WIDTHS[:b]), sum(BANK_WIDTHS[: b + 1])) for b in range(len(BANK_WIDTHS))]
-        for b, bank in enumerate(banks):
-            cols = bank_cols[b]
+        score_banks = [psum.tile([P, w], F32, name=f"scores{b}", tag=f"scores{b}") for b, w in enumerate(SCORE_WIDTHS)]
+        score_cols = [slice(sum(SCORE_WIDTHS[:b]), sum(SCORE_WIDTHS[: b + 1])) for b in range(len(SCORE_WIDTHS))]
+        for bank, cols in zip(score_banks, score_cols):
             nc.tensor.matmul_mx(
                 out=bank[:],
                 lhsT=states_w[:].bitcast(FP8X4),
                 lhsT_scale=states_sc[:],
                 rhs=tags_w[:, cols].bitcast(FP8X4),
-                rhs_scale=tags_sc[8:P, cols],
+                rhs_scale=tags_sc[TAGS_FIRST:P, cols],
                 start=True,
                 stop=False,
             )
         a = sb.tile([P, T], F32, align_bytes=64)
-        for b, bank in enumerate(banks):
-            cols = bank_cols[b]
+        for b, (bank, cols) in enumerate(zip(score_banks, score_cols)):
             nc.tensor.matmul_mx(
                 out=bank[:],
                 lhsT=qv_w[:].bitcast(FP8X4),
                 lhsT_scale=qv_sc[:],
                 rhs=keys_w[:, 2 * cols.start : 2 * cols.stop].bitcast(FP4X4),
-                rhs_scale=keys_sc[:, cols],
+                rhs_scale=keys_sc[KEYS_FIRST:P, cols],
                 start=False,
                 stop=True,
             )
@@ -145,47 +159,63 @@ def tile_attend_highlow_madeparts_kernel(
             else:
                 nc.vector.tensor_copy(out=a[:, cols], in_=bank[:])
 
-        halves = [slice(h * LIST_COLS // 2, (h + 1) * LIST_COLS // 2) for h in range(2)]
+        list_halves = [slice(h * LIST_COLS // 2, (h + 1) * LIST_COLS // 2) for h in range(2)]
         x = [sb.tile([P, HALF], F32, name=f"x{h}") for h in range(2)]
-        y = [sb.tile([P, HALF], F32, name="y")]
+        y_first = sb.tile([P, HALF], F32, tag="y")
         hi = [sb.tile([P, HALF], F32, name=f"hi{h}") for h in range(2)]
-        lo_all = sb.tile([P, SLOTS], F32)
-        lo = [lo_all[:, h * HALF : (h + 1) * HALF] for h in range(2)]
-        nc.vector.tensor_copy(x[0][:], a[:].indirect(idx[:, halves[0]]))
-        nc.scalar.activation(y[0][:], a[:].indirect(idx2[:, halves[0]]), COPY)
-        nc.scalar.activation(x[1][:], a[:].indirect(idx[:, halves[1]]), COPY)
-        for h in range(2):
-            if h == 1:
-                y.append(sb.tile([P, HALF], F32, name="y"))
-                nc.scalar.activation(y[1][:], a[:].indirect(idx2[:, halves[1]]), COPY)
-            nc.vector.tensor_tensor(hi[h][:], x[h][:], y[h][:], ALU.max)
-            nc.vector.tensor_tensor(lo[h], x[h][:], y[h][:], ALU.min)
-            nc.vector.tensor_copy(f1[:].indirect(idx3[:, halves[h]]), hi[h][:])
-        nc.vector.tensor_copy(f2[:].indirect(idx4[:]), lo_all[:])
+        lo = sb.tile([P, SLOTS], F32)
 
-        turned = sb.tile([P, 768], F32, align_bytes=64)
-        a_f1 = [psum.tile([P, 512], F32, name=f"back{b}") for b in range(2)]
-        fwd = [psum.tile([P, 256], F32, name=f"fwd{b}", tag=f"scores{b}") for b in range(3)]
-        for b in range(3):
-            for j in range(2):
-                cols = slice(256 * b + P * j, 256 * b + P * (j + 1))
-                nc.tensor.matmul(fwd[b][:, P * j : P * (j + 1)], a[:, cols], ident[:], start=(j == 0), stop=False, is_transpose=True)
-        for b in range(3):
-            for j in range(2):
-                cols = slice(256 * b + P * j, 256 * b + P * (j + 1))
-                nc.tensor.matmul(fwd[b][:, P * j : P * (j + 1)], f1[:, cols], ident[:], start=False, stop=(j == 1), is_transpose=True)
-            nc.scalar.copy(out=turned[:, 256 * b : 256 * (b + 1)], in_=fwd[b][:])
-        for c in range(6):
-            nc.tensor.transpose(a_f1[c // 4][:, P * (c % 4) : P * (c % 4 + 1)], turned[:, P * c : P * (c + 1)], ident[:])
+        def order_and_scatter_hi(h, y_half):
+            nc.vector.tensor_tensor(hi[h][:], x[h][:], y_half[:], ALU.max)
+            nc.vector.tensor_tensor(lo[:, h * HALF : (h + 1) * HALF], x[h][:], y_half[:], ALU.min)
+            nc.vector.tensor_copy(f1[:].indirect(idx3[:, list_halves[h]]), hi[h][:])
+
+        nc.vector.tensor_copy(y_first[:], a[:].indirect(idx2[:, list_halves[0]]))
+        for h in range(2):
+            nc.scalar.activation(x[h][:], a[:].indirect(idx[:, list_halves[h]]), COPY)
+        order_and_scatter_hi(0, y_first)
+        y_second = sb.tile([P, HALF], F32, tag="y")
+        nc.scalar.activation(y_second[:], a[:].indirect(idx2[:, list_halves[1]]), COPY)
+        order_and_scatter_hi(1, y_second)
+        nc.vector.tensor_copy(f2[:].indirect(idx4[:]), lo[:])
+
+        turned = sb.tile([P, VECTOR_COLS], F32, align_bytes=64)
+        a_f1_banks = [psum.tile([P, PSUM_BANK], F32, name=f"back{b}") for b in range(2)]
+        turn_banks = [
+            psum.tile([P, TURN_COLS], F32, name=f"turn{b}", tag=f"scores{b}") for b in range(VECTOR_COLS // TURN_COLS)
+        ]
+        blocks = TURN_COLS // P
+
+        def add_transposes(b, src, opens):
+            for j in range(blocks):
+                nc.tensor.matmul(
+                    turn_banks[b][:, P * j : P * (j + 1)],
+                    src[:, TURN_COLS * b + P * j : TURN_COLS * b + P * (j + 1)],
+                    ident[:],
+                    start=(opens and j == 0),
+                    stop=(not opens and j == blocks - 1),
+                    is_transpose=True,
+                )
+
+        for b in range(len(turn_banks)):
+            add_transposes(b, a, True)
+        for b in range(len(turn_banks)):
+            add_transposes(b, f1, False)
+            nc.scalar.copy(out=turned[:, TURN_COLS * b : TURN_COLS * (b + 1)], in_=turn_banks[b][:])
+        for col in range(0, VECTOR_COLS, P):
+            b, at = divmod(col, PSUM_BANK)
+            nc.tensor.transpose(a_f1_banks[b][:, at : at + P], turned[:, col : col + P], ident[:])
+
         cc = sb.tile([P, T], F32, align_bytes=64)
-        a_f1_rest = sb.tile([P, 256], F32, align_bytes=64)
-        nc.gpsimd.tensor_tensor(a_f1_rest[:], a[:, 768:T], f1[:, 768:T], ALU.add)
-        nc.gpsimd.tensor_tensor(cc[:, 768:T], a_f1_rest[:], f2[:, 768:T], ALU.subtract)
-        nc.vector.tensor_tensor(cc[:, 0:512], a_f1[0][:], f2[:, 0:512], ALU.subtract)
-        nc.vector.tensor_tensor(cc[:, 512:768], a_f1[1][:, 0:256], f2[:, 512:768], ALU.subtract)
+        a_f1_rest = sb.tile([P, T - VECTOR_COLS], F32, align_bytes=64)
+        nc.gpsimd.tensor_tensor(a_f1_rest[:], a[:, VECTOR_COLS:T], f1[:, VECTOR_COLS:T], ALU.add)
+        nc.gpsimd.tensor_tensor(cc[:, VECTOR_COLS:T], a_f1_rest[:], f2[:, VECTOR_COLS:T], ALU.subtract)
+        for b, bank in enumerate(a_f1_banks):
+            cols = slice(PSUM_BANK * b, min(PSUM_BANK * (b + 1), VECTOR_COLS))
+            nc.vector.tensor_tensor(cc[:, cols], bank[:, 0 : cols.stop - cols.start], f2[:, cols], ALU.subtract)
 
         res = [sb.tile([P, HALF], F32, name=f"res{h}") for h in range(2)]
-        nc.vector.tensor_copy(res[0][:], cc[:].indirect(idx[:, halves[0]]))
-        nc.scalar.activation(res[1][:], cc[:].indirect(idx[:, halves[1]]), COPY)
+        nc.vector.tensor_copy(res[0][:], cc[:].indirect(idx[:, list_halves[0]]))
+        nc.scalar.activation(res[1][:], cc[:].indirect(idx[:, list_halves[1]]), COPY)
         nc.sync.dma_start(out=out[:, 0:HALF], in_=res[0][:])
         nc.scalar.dma_start(out=out[:, HALF:SLOTS], in_=res[1][:])

from contextlib import ExitStack

import concourse.mybir as mybir
from concourse.masks import make_identity

D, K, T, SLOTS, Q = 512, 512, 1024, 512, 128
FLOPS = 2 * D * K * Q + 2 * K * Q * T + 2 * D * Q * T

F32 = mybir.dt.float32
BF16 = mybir.dt.bfloat16
I32 = mybir.dt.int32
U32 = mybir.dt.uint32
U16 = mybir.dt.uint16
U8 = mybir.dt.uint8
FP8X4 = mybir.dt.float8_e4m3fn_x4
FP4X4 = mybir.dt.float4_e2m1fn_x4
ALU = mybir.AluOpType
COPY = mybir.ActivationFunctionType.Copy

P = 128
PACK = 4
QUADRANT = 32
QUADRANT_ROWS = 4
PSUM_BANK = 512
LIST_COLS = SLOTS // 16
HALF = SLOTS // 2

WQ_FIRST, TAGS_FIRST, KEYS_FIRST = 4, 8, 0

SCALAR_DEAL = 48
SCORE_WIDTHS = (256, 256, 256, 128, 128)
VECTOR_COLS = 768
TURN_COLS = 256


def load_scale_rows(queue, plane, scales, quadrants, first):
    for g in quadrants:
        queue.dma_start(
            out=plane[:].bitcast(I32)[QUADRANT * g + first : QUADRANT * g + first + QUADRANT_ROWS, :],
            in_=scales[0].bitcast(I32)[QUADRANT_ROWS * g : QUADRANT_ROWS * (g + 1), :],
        )


def fp8_words(words):
    return words[0].rearrange("p n t -> p (n t)").bitcast(I32)


def tile_attend_highlow_madeparts_kernel(
    tc, states, wq_words, wq_scales, keys_words, keys_scales, tags_words, tags_scales, offs, offs2, offs3, offs4, out
):
    nc = tc.nc
    with ExitStack() as ctx:
        sb = ctx.enter_context(tc.tile_pool(name="sb", bufs=1))
        psum = ctx.enter_context(tc.psum_pool(name="psum", bufs=1))

        wq_sc_raw = sb.tile([P, K], U8, align_bytes=64)
        keys_sc = sb.tile([P, T], U8, align_bytes=64)
        tags_sc = sb.tile([P, T], U8, align_bytes=64)
        nc.gpsimd.memset(wq_sc_raw[:].bitcast(I32), 0)
        nc.gpsimd.memset(tags_sc[:].bitcast(I32), 0)
        nc.vector.memset(keys_sc[:].bitcast(I32), 0)

        states_raw = sb.tile([P, PACK, Q], F32, align_bytes=64)
        wq_raw = sb.tile([P, K], U32, align_bytes=64, tag="wq_raw_then_f1")
        tags_w = sb.tile([P, T], U32, align_bytes=64)
        keys_w = sb.tile([P, 2 * T], U8, align_bytes=64)
        nc.sync.dma_start(out=states_raw[:], in_=states.rearrange("(p j) q -> p j q", j=PACK))
        load_scale_rows(nc.sync, wq_sc_raw, wq_scales, (0, 1, 2, 3), WQ_FIRST)
        nc.sync.dma_start(out=wq_raw[:].bitcast(I32), in_=fp8_words(wq_words))
        load_scale_rows(nc.gpsimd, tags_sc, tags_scales, (3,), TAGS_FIRST)
        load_scale_rows(nc.sync, tags_sc, tags_scales, (0,), TAGS_FIRST)
        nc.sync.dma_start(out=tags_w[:].bitcast(I32), in_=fp8_words(tags_words))
        load_scale_rows(nc.sync, tags_sc, tags_scales, (1, 2), TAGS_FIRST)
        load_scale_rows(nc.sync, keys_sc, keys_scales, (0,), KEYS_FIRST)
        nc.sync.dma_start(out=keys_w[:].bitcast(I32), in_=keys_words[0].bitcast(I32))
        load_scale_rows(nc.sync, keys_sc, keys_scales, (1, 2, 3), KEYS_FIRST)
        lists = []
        for name, src in (("idx", offs), ("idx2", offs2), ("idx3", offs3), ("idx4", offs4)):
            list_tile = sb.tile([P, LIST_COLS], U16, name=name)
            nc.sync.dma_start(list_tile[:], src)
            lists.append(list_tile)
        idx, idx2, idx3, idx4 = lists

        ident = sb.tile([P, P], F32, align_bytes=64)
        nc.vector.memset(ident[:], 0.0)
        make_identity(nc, ident[:], nomemset=True)
        f2 = sb.tile([P, T], F32, align_bytes=64)
        nc.vector.memset(f2[:, 0 : T - 1], 0.0)
        nc.vector.memset(f2[:, T - 1 : T], 0.0)

        wq_sc = sb.tile([P, K], U8, align_bytes=64)
        nc.vector.tensor_copy(
            out=wq_sc[:].rearrange("p (t m) -> p t m", t=PACK), in_=wq_sc_raw[:].rearrange("p (m t) -> p t m", t=PACK)
        )
        wq_w = sb.tile([P, K], U32, align_bytes=64)
        dealt = wq_w[:].rearrange("p (t m) -> p m t", t=PACK)
        undealt = wq_raw[:].rearrange("p (m t) -> p m t", t=PACK)
        nc.scalar.copy(out=dealt[:, 0:SCALAR_DEAL, :], in_=undealt[:, 0:SCALAR_DEAL, :])

        states_bf = sb.tile([P, Q * PACK], BF16, align_bytes=64)
        nc.vector.tensor_copy(
            out=states_bf[:].rearrange("p (c i j) -> p c j i", i=4, j=PACK),
            in_=states_raw[:].rearrange("p j (c i) -> p c j i", i=4),
        )
        states_w = sb.tile([P, Q], U32, align_bytes=64)
        states_sc = sb.tile([P, Q], U8, align_bytes=64)
        nc.vector.quantize_mx(out=states_w[:].bitcast(FP8X4), scales=states_sc[:], in_=states_bf[:])

        nc.vector.tensor_copy(
            out=dealt[:, SCALAR_DEAL:P, :].bitcast(I32), in_=undealt[:, SCALAR_DEAL:P, :].bitcast(I32)
        )

        f1 = sb.tile([P, T], F32, align_bytes=64, tag="wq_raw_then_f1")
        nc.vector.memset(f1[:], 0.0)

        qv_ps = psum.tile([P, PACK, Q], F32)
        for t in range(PACK):
            places = slice(t * P, (t + 1) * P)
            nc.tensor.matmul_mx(
                out=qv_ps[:, t, :],
                lhsT=wq_w[:, places].bitcast(FP8X4),
                lhsT_scale=wq_sc[WQ_FIRST:P, places],
                rhs=states_w[:].bitcast(FP8X4),
                rhs_scale=states_sc[:],
                start=True,
                stop=True,
            )
        qv_bf = sb.tile([P, Q * PACK], BF16, align_bytes=64)
        nc.scalar.copy(out=qv_bf[:].rearrange("p (q t) -> p q t", t=PACK), in_=qv_ps[:].rearrange("p t q -> p q t"))
        qv_w = sb.tile([P, Q], U32, align_bytes=64)
        qv_sc = sb.tile([P, Q], U8, align_bytes=64)
        nc.vector.quantize_mx(out=qv_w[:].bitcast(FP8X4), scales=qv_sc[:], in_=qv_bf[:])

        score_banks = [psum.tile([P, w], F32, name=f"scores{b}", tag=f"scores{b}") for b, w in enumerate(SCORE_WIDTHS)]
        score_cols = [slice(sum(SCORE_WIDTHS[:b]), sum(SCORE_WIDTHS[: b + 1])) for b in range(len(SCORE_WIDTHS))]
        for bank, cols in zip(score_banks, score_cols):
            nc.tensor.matmul_mx(
                out=bank[:],
                lhsT=states_w[:].bitcast(FP8X4),
                lhsT_scale=states_sc[:],
                rhs=tags_w[:, cols].bitcast(FP8X4),
                rhs_scale=tags_sc[TAGS_FIRST:P, cols],
                start=True,
                stop=False,
            )
        a = sb.tile([P, T], F32, align_bytes=64)
        for b, (bank, cols) in enumerate(zip(score_banks, score_cols)):
            nc.tensor.matmul_mx(
                out=bank[:],
                lhsT=qv_w[:].bitcast(FP8X4),
                lhsT_scale=qv_sc[:],
                rhs=keys_w[:, 2 * cols.start : 2 * cols.stop].bitcast(FP4X4),
                rhs_scale=keys_sc[KEYS_FIRST:P, cols],
                start=False,
                stop=True,
            )
            if b % 2 == 0:
                nc.scalar.copy(out=a[:, cols], in_=bank[:])
            else:
                nc.vector.tensor_copy(out=a[:, cols], in_=bank[:])

        list_halves = [slice(h * LIST_COLS // 2, (h + 1) * LIST_COLS // 2) for h in range(2)]
        x = [sb.tile([P, HALF], F32, name=f"x{h}") for h in range(2)]
        y_first = sb.tile([P, HALF], F32, tag="y")
        hi = [sb.tile([P, HALF], F32, name=f"hi{h}") for h in range(2)]
        lo = sb.tile([P, SLOTS], F32)

        def order_and_scatter_hi(h, y_half):
            nc.vector.tensor_tensor(hi[h][:], x[h][:], y_half[:], ALU.max)
            nc.vector.tensor_tensor(lo[:, h * HALF : (h + 1) * HALF], x[h][:], y_half[:], ALU.min)
            nc.vector.tensor_copy(f1[:].indirect(idx3[:, list_halves[h]]), hi[h][:])

        nc.vector.tensor_copy(y_first[:], a[:].indirect(idx2[:, list_halves[0]]))
        for h in range(2):
            nc.scalar.activation(x[h][:], a[:].indirect(idx[:, list_halves[h]]), COPY)
        order_and_scatter_hi(0, y_first)
        y_second = sb.tile([P, HALF], F32, tag="y")
        nc.scalar.activation(y_second[:], a[:].indirect(idx2[:, list_halves[1]]), COPY)
        order_and_scatter_hi(1, y_second)
        nc.vector.tensor_copy(f2[:].indirect(idx4[:]), lo[:])

        turned = sb.tile([P, VECTOR_COLS], F32, align_bytes=64)
        a_f1_banks = [psum.tile([P, PSUM_BANK], F32, name=f"back{b}") for b in range(2)]
        turn_banks = [
            psum.tile([P, TURN_COLS], F32, name=f"turn{b}", tag=f"scores{b}") for b in range(VECTOR_COLS // TURN_COLS)
        ]
        blocks = TURN_COLS // P

        def add_transposes(b, src, opens):
            for j in range(blocks):
                nc.tensor.matmul(
                    turn_banks[b][:, P * j : P * (j + 1)],
                    src[:, TURN_COLS * b + P * j : TURN_COLS * b + P * (j + 1)],
                    ident[:],
                    start=(opens and j == 0),
                    stop=(not opens and j == blocks - 1),
                    is_transpose=True,
                )

        for b in range(len(turn_banks)):
            add_transposes(b, a, True)
        for b in range(len(turn_banks)):
            add_transposes(b, f1, False)
            nc.scalar.copy(out=turned[:, TURN_COLS * b : TURN_COLS * (b + 1)], in_=turn_banks[b][:])
        for col in range(0, VECTOR_COLS, P):
            b, at = divmod(col, PSUM_BANK)
            nc.tensor.transpose(a_f1_banks[b][:, at : at + P], turned[:, col : col + P], ident[:])

        cc = sb.tile([P, T], F32, align_bytes=64)
        a_f1_rest = sb.tile([P, T - VECTOR_COLS], F32, align_bytes=64)
        nc.gpsimd.tensor_tensor(a_f1_rest[:], a[:, VECTOR_COLS:T], f1[:, VECTOR_COLS:T], ALU.add)
        nc.gpsimd.tensor_tensor(cc[:, VECTOR_COLS:T], a_f1_rest[:], f2[:, VECTOR_COLS:T], ALU.subtract)
        for b, bank in enumerate(a_f1_banks):
            cols = slice(PSUM_BANK * b, min(PSUM_BANK * (b + 1), VECTOR_COLS))
            nc.vector.tensor_tensor(cc[:, cols], bank[:, 0 : cols.stop - cols.start], f2[:, cols], ALU.subtract)

        res = [sb.tile([P, HALF], F32, name=f"res{h}") for h in range(2)]
        nc.vector.tensor_copy(res[0][:], cc[:].indirect(idx[:, list_halves[0]]))
        nc.scalar.activation(res[1][:], cc[:].indirect(idx[:, list_halves[1]]), COPY)
        nc.sync.dma_start(out=out[:, 0:HALF], in_=res[0][:])
        nc.scalar.dma_start(out=out[:, HALF:SLOTS], in_=res[1][:])
